import numpy as np
import ml_dtypes

BF16 = ml_dtypes.bfloat16


def bf(x):
    return np.asarray(x, np.float32).astype(BF16)


def f32(x):
    return np.asarray(x, np.float32)


def f64(x):
    return np.asarray(x).astype(np.float64)


def striped(idx):
    return np.concatenate([l.reshape(-1, 16).T for l in idx])


def rows(idx, k):
    return np.tile(np.repeat(idx, 16, axis=0), (k // (16 * 8), 1))


def look(tab, idx):
    return np.take_along_axis(f64(tab), rows(idx, len(tab)), axis=1)


K, S, V, N, M = 256, 2048, 1024, 1024, 256


def setup_inputs():
    return {"tab": bf(np.random.standard_normal((K, S))), "w": bf(np.random.standard_normal((K, M)) / np.sqrt(K)), "offs": striped(np.random.randint(0, S, (8, N)))}


def reference(tab, w, offs):
    idx = np.stack([g.T.reshape(-1) for g in np.split(offs, 8)])
    t = look(tab, idx)
    x = t
    y = f64(w).T @ x
    return y

@@ -1,0 +1,59 @@
+import concourse.mybir as mybir
+
+BF16, F32, U16 = mybir.dt.bfloat16, mybir.dt.float32, mybir.dt.uint16
+
+P = 128
+PIECE = 512
+PER_COLUMN = 16
+
+FLOPS = 2 * 256 * 256 * 1024
+
+
+def tile_lookup_dec_copy_none_kernel(tc, tab, w, offs, out):
+    nc = tc.nc
+    n_rows, n_codewords = tab.shape
+    n_out, n_codes = out.shape
+    n_blocks = n_rows // P
+    n_m = n_out // P
+    n_pieces = n_codes // PIECE
+
+    with (
+        tc.tile_pool(name="held", bufs=1) as held,
+        tc.psum_pool(name="psum", bufs=1) as psum,
+    ):
+        offsets = held.tile([P, n_codes // PER_COLUMN], U16, name="offsets")
+        nc.sync.dma_start(offsets[:], offs)
+
+        windows = []
+        for b in range(n_blocks):
+            window = held.tile([P, n_codewords], BF16, name=f"window{b}")
+            nc.sync.dma_start(window[:], tab[b * P : (b + 1) * P, :])
+            windows.append(window)
+
+        weights = held.tile([P, n_blocks, n_out], BF16, name="weights")
+        nc.sync.dma_start(weights[:], w.rearrange("(b p) m -> p b m", p=P))
+
+        for piece in range(n_pieces):
+            codes = slice(piece * PIECE, (piece + 1) * PIECE)
+            columns = slice(codes.start // PER_COLUMN, codes.stop // PER_COLUMN)
+
+            picked = []
+            for b in range(n_blocks):
+                x = held.tile([P, PIECE], BF16, name=f"x{piece}_{b}")
+                nc.vector.tensor_copy(x[:], windows[b][:].indirect(offsets[:, columns]))
+                picked.append(x)
+
+            for m in range(n_m):
+                rows = slice(m * P, (m + 1) * P)
+                product = psum.tile([P, PIECE], F32, name=f"product{piece}_{m}")
+                for b in range(n_blocks):
+                    nc.tensor.matmul(
+                        product[:],
+                        weights[:, b, rows],
+                        picked[b][:],
+                        start=b == 0,
+                        stop=b == n_blocks - 1,
+                    )
+                staged = held.tile([P, PIECE], F32, name=f"staged{piece}_{m}")
+                nc.scalar.copy(staged[:], product[:])
+                nc.sync.dma_start(out[rows, codes], staged[:])

@@ -36,24 +36,24 @@ def tile_lookup_dec_copy_none_kernel(tc, tab, w, offs, out):
         for piece in range(n_pieces):
             codes = slice(piece * PIECE, (piece + 1) * PIECE)
             columns = slice(codes.start // PER_COLUMN, codes.stop // PER_COLUMN)
+            products = [psum.tile([P, PIECE], F32, name=f"product{piece}_{m}") for m in range(n_m)]
 
-            picked = []
             for b in range(n_blocks):
-                x = held.tile([P, PIECE], BF16, name=f"x{piece}_{b}")
-                nc.vector.tensor_copy(x[:], windows[b][:].indirect(offsets[:, columns]))
-                picked.append(x)
-
-            for m in range(n_m):
-                rows = slice(m * P, (m + 1) * P)
-                product = psum.tile([P, PIECE], F32, name=f"product{piece}_{m}")
-                for b in range(n_blocks):
+                picked = held.tile([P, PIECE], BF16, name=f"picked{piece}_{b}")
+                nc.vector.tensor_copy(picked[:], windows[b][:].indirect(offsets[:, columns]))
+                for m in range(n_m):
                     nc.tensor.matmul(
-                        product[:],
-                        weights[:, b, rows],
-                        picked[b][:],
+                        products[m][:],
+                        weights[:, b, m * P : (m + 1) * P],
+                        picked[:],
                         start=b == 0,
                         stop=b == n_blocks - 1,
                     )
+
+            for m in range(n_m):
                 staged = held.tile([P, PIECE], F32, name=f"staged{piece}_{m}")
-                nc.scalar.copy(staged[:], product[:])
-                nc.sync.dma_start(out[rows, codes], staged[:])
+                if piece == n_pieces - 1 and m % 2 == 1:
+                    nc.vector.tensor_copy(staged[:], products[m][:])
+                else:
+                    nc.scalar.copy(staged[:], products[m][:])
+                nc.sync.dma_start(out[m * P : (m + 1) * P, codes], staged[:])

@@ -24,36 +24,39 @@ def tile_lookup_dec_copy_none_kernel(tc, tab, w, offs, out):
         offsets = held.tile([P, n_codes // PER_COLUMN], U16, name="offsets")
         nc.sync.dma_start(offsets[:], offs)
 
-        windows = []
-        for b in range(n_blocks):
-            window = held.tile([P, n_codewords], BF16, name=f"window{b}")
-            nc.sync.dma_start(window[:], tab[b * P : (b + 1) * P, :])
-            windows.append(window)
-
+        windows = [held.tile([P, n_codewords], BF16, name=f"window{b}") for b in range(n_blocks)]
         weights = held.tile([P, n_blocks, n_out], BF16, name="weights")
-        nc.sync.dma_start(weights[:], w.rearrange("(b p) m -> p b m", p=P))
+        for b in range(n_blocks):
+            nc.sync.dma_start(windows[b][:], tab[b * P : (b + 1) * P, :])
+            if b == 0:
+                nc.sync.dma_start(weights[:], w.rearrange("(b p) m -> p b m", p=P))
 
-        for piece in range(n_pieces):
-            codes = slice(piece * PIECE, (piece + 1) * PIECE)
-            columns = slice(codes.start // PER_COLUMN, codes.stop // PER_COLUMN)
-            products = [psum.tile([P, PIECE], F32, name=f"product{piece}_{m}") for m in range(n_m)]
+        products = [
+            [psum.tile([P, PIECE], F32, name=f"product{piece}_{m}") for m in range(n_m)]
+            for piece in range(n_pieces)
+        ]
 
-            for b in range(n_blocks):
-                picked = held.tile([P, PIECE], BF16, name=f"picked{piece}_{b}")
+        for b in range(n_blocks):
+            for piece in range(n_pieces):
+                columns = slice(piece * PIECE // PER_COLUMN, (piece + 1) * PIECE // PER_COLUMN)
+                picked = held.tile([P, PIECE], BF16, name=f"picked{b}_{piece}")
                 nc.vector.tensor_copy(picked[:], windows[b][:].indirect(offsets[:, columns]))
                 for m in range(n_m):
                     nc.tensor.matmul(
-                        products[m][:],
+                        products[piece][m][:],
                         weights[:, b, m * P : (m + 1) * P],
                         picked[:],
                         start=b == 0,
                         stop=b == n_blocks - 1,
                     )
 
+        for piece in range(n_pieces):
             for m in range(n_m):
                 staged = held.tile([P, PIECE], F32, name=f"staged{piece}_{m}")
+                place = out[m * P : (m + 1) * P, piece * PIECE : (piece + 1) * PIECE]
                 if piece == n_pieces - 1 and m % 2 == 1:
-                    nc.vector.tensor_copy(staged[:], products[m][:])
+                    nc.vector.tensor_copy(staged[:], products[piece][m][:])
+                    nc.sync.dma_start(place, staged[:])
                 else:
-                    nc.scalar.copy(staged[:], products[m][:])
-                nc.sync.dma_start(out[m * P : (m + 1) * P, codes], staged[:])
+                    nc.scalar.copy(staged[:], products[piece][m][:])
+                    nc.scalar.dma_start(place, staged[:])

@@ -53,10 +53,6 @@ def tile_lookup_dec_copy_none_kernel(tc, tab, w, offs, out):
         for piece in range(n_pieces):
             for m in range(n_m):
                 staged = held.tile([P, PIECE], F32, name=f"staged{piece}_{m}")
+                nc.scalar.copy(staged[:], products[piece][m][:])
                 place = out[m * P : (m + 1) * P, piece * PIECE : (piece + 1) * PIECE]
-                if piece == n_pieces - 1 and m % 2 == 1:
-                    nc.vector.tensor_copy(staged[:], products[piece][m][:])
-                    nc.sync.dma_start(place, staged[:])
-                else:
-                    nc.scalar.copy(staged[:], products[piece][m][:])
-                    nc.scalar.dma_start(place, staged[:])
+                nc.sync.dma_start(place, staged[:])

@@ -27,7 +27,8 @@ def tile_lookup_dec_copy_none_kernel(tc, tab, w, offs, out):
         windows = [held.tile([P, n_codewords], BF16, name=f"window{b}") for b in range(n_blocks)]
         weights = held.tile([P, n_blocks, n_out], BF16, name="weights")
         for b in range(n_blocks):
-            nc.sync.dma_start(windows[b][:], tab[b * P : (b + 1) * P, :])
+            queue = nc.scalar if b == 0 else nc.sync
+            queue.dma_start(windows[b][:], tab[b * P : (b + 1) * P, :])
             if b == 0:
                 nc.sync.dma_start(weights[:], w.rearrange("(b p) m -> p b m", p=P))
 

import concourse.mybir as mybir

BF16, F32, U16 = mybir.dt.bfloat16, mybir.dt.float32, mybir.dt.uint16

P = 128
PIECE = 512
PER_COLUMN = 16

FLOPS = 2 * 256 * 256 * 1024


def tile_lookup_dec_copy_none_kernel(tc, tab, w, offs, out):
    nc = tc.nc
    n_rows, n_codewords = tab.shape
    n_out, n_codes = out.shape
    n_blocks = n_rows // P
    n_m = n_out // P
    n_pieces = n_codes // PIECE

    with (
        tc.tile_pool(name="held", bufs=1) as held,
        tc.psum_pool(name="psum", bufs=1) as psum,
    ):
        offsets = held.tile([P, n_codes // PER_COLUMN], U16, name="offsets")
        nc.sync.dma_start(offsets[:], offs)

        windows = [held.tile([P, n_codewords], BF16, name=f"window{b}") for b in range(n_blocks)]
        weights = held.tile([P, n_blocks, n_out], BF16, name="weights")
        for b in range(n_blocks):
            queue = nc.scalar if b == 0 else nc.sync
            queue.dma_start(windows[b][:], tab[b * P : (b + 1) * P, :])
            if b == 0:
                nc.sync.dma_start(weights[:], w.rearrange("(b p) m -> p b m", p=P))

        products = [
            [psum.tile([P, PIECE], F32, name=f"product{piece}_{m}") for m in range(n_m)]
            for piece in range(n_pieces)
        ]

        for b in range(n_blocks):
            for piece in range(n_pieces):
                columns = slice(piece * PIECE // PER_COLUMN, (piece + 1) * PIECE // PER_COLUMN)
                picked = held.tile([P, PIECE], BF16, name=f"picked{b}_{piece}")
                nc.vector.tensor_copy(picked[:], windows[b][:].indirect(offsets[:, columns]))
                for m in range(n_m):
                    nc.tensor.matmul(
                        products[piece][m][:],
                        weights[:, b, m * P : (m + 1) * P],
                        picked[:],
                        start=b == 0,
                        stop=b == n_blocks - 1,
                    )

        for piece in range(n_pieces):
            for m in range(n_m):
                staged = held.tile([P, PIECE], F32, name=f"staged{piece}_{m}")
                nc.scalar.copy(staged[:], products[piece][m][:])
                place = out[m * P : (m + 1) * P, piece * PIECE : (piece + 1) * PIECE]
                nc.sync.dma_start(place, staged[:])
